import numpy as np
import ml_dtypes


def mxq(x, axis, fmt="e4m3"):
    dtype, down = {"e4m3": (ml_dtypes.float8_e4m3fn, 7), "e5m2": (ml_dtypes.float8_e5m2, 14)}[fmt]
    v = np.moveaxis(np.asarray(x, np.float32).astype(ml_dtypes.bfloat16).astype(np.float64), axis, -1)
    blocks = v.reshape(v.shape[:-1] + (-1, 32))
    amax = np.abs(blocks).max(-1, keepdims=True)
    byte = np.maximum(np.where(amax > 0, np.frexp(amax)[1] - 1 + 127, 0) - down, 1)
    scale = np.exp2(byte - 127.0)
    codes = (blocks / scale).astype(np.float32).astype(dtype).astype(np.float64)
    return np.moveaxis((codes * scale).reshape(v.shape), -1, axis)


WIDE = False


def mx_kscale(k):
    if not WIDE:
        return np.ones(k)
    levels = np.array([10, -10, 5, -5, 0])
    if k % 512:
        return np.exp2(np.random.permutation(np.resize(levels, k // 32))).repeat(32)
    a = np.empty((k // 512, 16))
    for p in range(k // 512):
        a[p, :8] = np.random.permutation(np.resize(levels, 8))
        for g in range(8):
            far = levels[np.abs(levels - a[p, g]) >= 10]
            a[p, g + 8] = far[np.random.randint(len(far))]
    return np.exp2(a.ravel()).repeat(32)


def f64(x):
    return np.asarray(x).astype(np.float64)


def striped(idx):
    return np.tile(idx.reshape(-1, 16).T, (8, 1)).astype(np.uint16)


def unstriped(offs):
    return offs[:16].T.reshape(-1).astype(np.int64)


E2M1 = np.array([0.0, 0.5, 1.0, 1.5, 2.0, 3.0, 4.0, 6.0, -0.0, -0.5, -1.0, -1.5, -2.0, -3.0, -4.0, -6.0])


def pack_weight(w, fmt):
    k, n = w.shape
    w = f64(np.asarray(w, np.float32).astype(ml_dtypes.bfloat16)).reshape(k // 32, 32, n)
    amax = np.abs(w).max(1)
    if fmt == "e4m3":
        byte = np.frexp(amax)[1] - 1 + 127 - 7
    else:
        mant, ex = np.frexp(amax / 6.0)
        byte = np.where(mant > 0.5, ex, ex - 1) + 127
    byte = np.clip(np.where(amax > 0, byte, 1), 1, 254)
    scaled = (w * np.exp2(127.0 - byte)[:, None, :]).reshape(k, n).astype(np.float32)
    by_word = np.ascontiguousarray(scaled.reshape(k // 512, 128, 4, n).transpose(0, 1, 3, 2))
    if fmt == "e4m3":
        words = by_word.astype(ml_dtypes.float8_e4m3fn).view(np.uint8)
    else:
        c = by_word.astype(ml_dtypes.float4_e2m1fn).view(np.uint8) & 0xF
        words = (c[..., 0::2] | (c[..., 1::2] << 4)).reshape(k // 512, 128, 2 * n)
    return np.ascontiguousarray(words), np.ascontiguousarray(byte.astype(np.uint8).reshape(k // 512, 16, n))


def unpack_weight(words, scales, fmt):
    g, _, n = scales.shape
    words = np.ascontiguousarray(words).reshape(g, 128, n, -1)
    if fmt == "e4m3":
        vals = words.view(ml_dtypes.float8_e4m3fn).astype(np.float64)
    else:
        nib = np.empty((g, 128, n, 4), np.uint8)
        nib[..., 0::2] = words & 0xF
        nib[..., 1::2] = words >> 4
        vals = E2M1[nib]
    vals = vals * np.repeat(np.exp2(scales.astype(np.float64) - 127.0), 8, axis=1)[..., None]
    return vals.transpose(0, 1, 3, 2).reshape(g * 512, n)


K, T, E, C, H, N = 512, 768, 2, 256, 512, 512


def by_expert(wq, xq):
    return np.concatenate([wq[e].T @ xq[:, e * C:(e + 1) * C] for e in range(E)], axis=1)


def setup_inputs():
    n = np.random.standard_normal
    v = mx_kscale(N)
    u = mx_kscale(H)
    slot_token = np.random.permutation(T)[:E * C]
    w_slot = np.random.uniform(0.2, 1.0, E * C)
    partner = np.random.permutation(T)[:E * C]
    dy = pack_weight(n((N, T)) * v[:, None], "e4m3")
    w2t = [pack_weight(m, "e4m3") for m in n((E, N, H)) / np.sqrt(N) / v[None, :, None] * u]
    w1t = [pack_weight(m, "e4m3") for m in n((E, H, K)) / np.sqrt(H) / u[None, :, None]]
    wpt = [pack_weight(m, "e4m3") for m in n((E, H, K)) / np.sqrt(H) / u[None, :, None]]
    return {
        "dy_words": dy[0],
        "dy_scales": dy[1],
        "w2t_words": np.stack([m[0] for m in w2t]),
        "w2t_scales": np.stack([m[1] for m in w2t]),
        "w1t_words": np.stack([m[0] for m in w1t]),
        "w1t_scales": np.stack([m[1] for m in w1t]),
        "wpt_words": np.stack([m[0] for m in wpt]),
        "wpt_scales": np.stack([m[1] for m in wpt]),
        "gate": (np.tile(w_slot, (128, 1))).astype(np.float32),
        "offs": striped(slot_token),
        "offs2": striped(partner),
    }


def reference(dy_words, dy_scales, w2t_words, w2t_scales, w1t_words, w1t_scales, wpt_words, wpt_scales, gate, offs, offs2):
    w2t = np.stack([unpack_weight(w2t_words[e], w2t_scales[e], "e4m3") for e in range(E)])
    w1t = np.stack([unpack_weight(w1t_words[e], w1t_scales[e], "e4m3") for e in range(E)])
    wpt = np.stack([unpack_weight(wpt_words[e], wpt_scales[e], "e4m3") for e in range(E)])
    idx, idx2 = unstriped(offs), unstriped(offs2)
    gq = unpack_weight(dy_words, dy_scales, "e4m3")[:, idx]
    dh = f64(gate[:1]) * by_expert(w2t, gq)
    dq = mxq(dh, 0, "e4m3")
    out = np.zeros((K, T))
    out[:, idx] = by_expert(w1t, dq)
    out[:, idx2] += by_expert(wpt, dq)
    return out

@@ -1,0 +1,194 @@
+from contextlib import ExitStack
+
+import concourse.mybir as mybir
+from concourse.masks import make_identity
+
+K, T, E, C, H, N = 512, 768, 2, 256, 512, 512
+S = E * C
+P = 128
+FLOPS = 3 * 2 * 512 * 512 * S
+
+F32 = mybir.dt.float32
+BF16 = mybir.dt.bfloat16
+I32 = mybir.dt.int32
+U32 = mybir.dt.uint32
+U16 = mybir.dt.uint16
+U8 = mybir.dt.uint8
+X4 = mybir.dt.float8_e4m3fn_x4
+COPY = mybir.ActivationFunctionType.Copy
+ADD = mybir.AluOpType.add
+
+CHUNKS = S // P
+KBLOCKS = K // P
+
+
+def tile_moe_dub_none_kernel(
+    tc, dy_words, dy_scales, w2t_words, w2t_scales, w1t_words, w1t_scales, wpt_words, wpt_scales, gate, offs, offs2, out
+):
+    nc = tc.nc
+    with ExitStack() as ctx:
+        sb = ctx.enter_context(tc.tile_pool(name="sb", bufs=1))
+        ps = ctx.enter_context(tc.psum_pool(name="ps", bufs=1))
+
+        def sbt(name, shape, dtype):
+            return sb.tile(shape, dtype, name=name, align_bytes=64)
+
+        idx = sb.tile([P, S // 16], U16, name="idx")
+        idx2 = sb.tile([P, S // 16], U16, name="idx2")
+        banks = [ps.tile([P, 512], F32, name="bank%d" % b) for b in range(8)]
+
+        dyw = sbt("dyw", [P, T], I32)
+        dys = sbt("dys", [P, T], U8)
+        w2w = [sbt("w2w%d" % e, [P, H], I32) for e in range(E)]
+        w1w = sbt("w1w", [P, E, K], I32)
+        wpw = sbt("wpw", [P, E, K], I32)
+        w2s = sbt("w2s", [P, E, H], U8)
+        w1s = sbt("w1s", [P, E, K], U8)
+        wps = sbt("wps", [P, E, K], U8)
+        gcol = sbt("gcol", [P, CHUNKS], F32)
+        ident = sbt("ident", [P, P], F32)
+        win = [[sbt("win%d_%d" % (a, b), [P, T], F32) for b in range(2)] for a in range(2)]
+
+        nc.gpsimd.memset(dys[:].bitcast(I32), 0)
+        nc.gpsimd.memset(w2s[:].bitcast(I32), 0)
+        nc.gpsimd.memset(w1s[:].bitcast(I32), 0)
+        nc.gpsimd.memset(wps[:].bitcast(I32), 0)
+        nc.vector.memset(win[0][0][:], 0.0)
+        nc.vector.memset(win[1][0][:], 0.0)
+        nc.vector.memset(win[0][1][:], 0.0)
+        make_identity(nc, ident[:])
+
+        def load_scales(queue, plane, scales):
+            rows = scales.rearrange("e s (q r) i -> r q (e s) i", r=4)
+            for r in range(4):
+                queue.dma_start(out=plane[:].bitcast(I32)[r:P:32], in_=rows[r].bitcast(I32))
+
+        def words_of(w):
+            return w.rearrange("e s p i d -> p (e s) (i d)").bitcast(I32)
+
+        nc.sync.dma_start(idx[:], offs)
+        dy_rows = dy_scales[0].rearrange("(q r) t -> r q t", r=4)
+        for r in range(4):
+            nc.scalar.dma_start(out=dys[:].bitcast(I32)[r:P:32], in_=dy_rows[r].bitcast(I32))
+        nc.sync.dma_start(out=dyw[:], in_=dy_words[0].rearrange("p t d -> p (t d)").bitcast(I32))
+        nc.sync.dma_start(out=w2w[0][:], in_=words_of(w2t_words)[:, 0, :])
+        with nc.allow_non_contiguous_dma(reason="one gate value a partition"):
+            nc.sync.dma_start(out=gcol[:], in_=gate[0:1, :].rearrange("o (c p) -> p (o c)", p=P))
+        load_scales(nc.sync, w2s, w2t_scales)
+        nc.sync.dma_start(out=w1w[:], in_=words_of(w1t_words))
+        load_scales(nc.sync, w1s, w1t_scales)
+        nc.sync.dma_start(out=w2w[1][:], in_=words_of(w2t_words)[:, 1, :])
+        nc.sync.dma_start(out=wpw[:], in_=words_of(wpt_words))
+        nc.sync.dma_start(idx2[:], offs2)
+        load_scales(nc.sync, wps, wpt_scales)
+
+        nc.scalar.activation(out=win[1][1][:], in_=win[0][0][:], func=COPY)
+
+        dq = sbt("dq", [P, S], U32)
+        dqs = sbt("dqs", [P, S], U8)
+        gw = [sbt("gw%d" % c, [P, P], U32) for c in range(CHUNKS)]
+        gs = [sbt("gs%d" % c, [P, P], U8) for c in range(CHUNKS)]
+        dh = [sbt("dh%d" % c, [P, H], BF16) for c in range(CHUNKS)]
+        dht = [sbt("dht%d" % c, [P, P * 4], BF16) for c in range(CHUNKS)]
+        lists = [idx, idx2]
+        words2 = [w1w, wpw]
+        scales2 = [w1s, wps]
+        src = [[sbt("src%d_%d" % (a, kb), [P, S], F32) for kb in range(KBLOCKS)] for a in range(2)]
+
+        def gather(c):
+            cols = idx[:, c * 8 : (c + 1) * 8]
+            nc.vector.tensor_copy(gs[c][:], dys[:].indirect(cols))
+            nc.vector.tensor_copy(gw[c][:], dyw[:].bitcast(U32).indirect(cols))
+
+        def first(c):
+            e = c * P // C
+            acc = banks[c % 2]
+            nc.tensor.matmul_mx(
+                out=acc[:], lhsT=gw[c][:].bitcast(X4), lhsT_scale=gs[c][:],
+                rhs=w2w[e][:].bitcast(X4), rhs_scale=w2s[:, e, :], start=True, stop=True,
+            )
+            nc.scalar.activation(
+                out=dh[c][:].rearrange("s (u p h) -> s u p h", u=2, h=2),
+                in_=acc[:].rearrange("s (p u h) -> s u p h", u=2, h=2),
+                func=COPY, scale=gcol[:, c : c + 1],
+            )
+
+        def turn(c):
+            bank = banks[2 + c % 2]
+            pairs = dh[c][:].bitcast(F32)
+            for u in range(2):
+                nc.tensor.transpose(bank[:, u * P : (u + 1) * P], pairs[:, u * P : (u + 1) * P], ident[:])
+            nc.scalar.copy(
+                out=dht[c][:].bitcast(F32).rearrange("p (s u) -> p s u", u=2),
+                in_=bank[:, 0 : 2 * P].rearrange("p (u s) -> p s u", u=2),
+            )
+            nc.vector.quantize_mx(out=dq[:, c * P : (c + 1) * P].bitcast(X4), scales=dqs[:, c * P : (c + 1) * P], in_=dht[c][:])
+
+        def second(a, kb, lo, hi, bank):
+            step = min(hi - lo, C)
+            for s0 in range(lo, hi, step):
+                e = s0 // C
+                nc.tensor.matmul_mx(
+                    out=bank[:, s0 - lo : s0 - lo + step],
+                    lhsT=words2[a][:, e, kb * P : (kb + 1) * P].bitcast(X4),
+                    lhsT_scale=scales2[a][:, e, kb * P : (kb + 1) * P],
+                    rhs=dq[:, s0 : s0 + step].bitcast(X4), rhs_scale=dqs[:, s0 : s0 + step],
+                    start=True, stop=True,
+                )
+            nc.scalar.copy(out=src[a][kb][:, lo:hi], in_=bank[:, 0 : hi - lo])
+            nc.vector.tensor_copy(win[a][kb % 2][:].indirect(lists[a][:, lo // 16 : hi // 16]), src[a][kb][:, lo:hi])
+
+        def add_on_tensor(kb):
+            half = T // 2
+            res = sbt("res%d" % kb, [P, T], F32)
+            for h in range(2):
+                turned = sbt("turned%d_%d" % (kb, h), [P, half], F32)
+                for j in range(half // P):
+                    cols = slice(h * half + j * P, h * half + (j + 1) * P)
+                    for a in range(2):
+                        nc.tensor.matmul(
+                            banks[h][:, j * P : (j + 1) * P], lhsT=win[a][kb % 2][:, cols], rhs=ident[:],
+                            is_transpose=True, start=(a == 0), stop=(a == 1),
+                        )
+                nc.scalar.copy(out=turned[:], in_=banks[h][:, 0:half])
+                for j in range(half // P):
+                    nc.tensor.transpose(banks[2 + h][:, j * P : (j + 1) * P], turned[:, j * P : (j + 1) * P], ident[:])
+                nc.scalar.copy(out=res[:, h * half : (h + 1) * half], in_=banks[2 + h][:, 0:half])
+            nc.sync.dma_start(out=out[kb * P : (kb + 1) * P, :], in_=res[:])
+
+        def add_on_vector(kb):
+            third = T // 3
+            for j in range(3):
+                cols = slice(j * third, (j + 1) * third)
+                res = sbt("res%d_%d" % (kb, j), [P, third], F32)
+                nc.vector.tensor_tensor(res[:], win[0][kb % 2][:, cols], win[1][kb % 2][:, cols], ADD)
+                queue = nc.scalar if j == 1 else nc.sync
+                queue.dma_start(out=out[kb * P : (kb + 1) * P, cols], in_=res[:])
+
+        for c in range(CHUNKS):
+            gather(c)
+        first(0)
+        first(1)
+        turn(0)
+        second(0, 0, 0, P, banks[4])
+        turn(1)
+        second(1, 0, 0, P, banks[5])
+        first(2)
+        second(0, 0, P, C, banks[6])
+        turn(2)
+        first(3)
+        second(1, 0, P, C, banks[7])
+        turn(3)
+        second(0, 1, 0, C, banks[3])
+        second(0, 0, C, S, banks[4])
+        second(1, 0, C, S, banks[5])
+        second(0, 1, C, S, banks[6])
+        second(1, 1, 0, S, banks[7])
+        add_on_tensor(0)
+        second(0, 2, 0, S, banks[4])
+        second(1, 2, 0, S, banks[5])
+        add_on_tensor(1)
+        second(0, 3, 0, S, banks[6])
+        second(1, 3, 0, S, banks[7])
+        add_on_tensor(2)
+        add_on_vector(3)

@@ -40,71 +40,77 @@ def tile_moe_dub_none_kernel(
         dyw = sbt("dyw", [P, T], I32)
         dys = sbt("dys", [P, T], U8)
         w2w = [sbt("w2w%d" % e, [P, H], I32) for e in range(E)]
-        w1w = sbt("w1w", [P, E, K], I32)
+        w1w = [sbt("w1w%d" % e, [P, K], I32) for e in range(E)]
         wpw = sbt("wpw", [P, E, K], I32)
         w2s = sbt("w2s", [P, E, H], U8)
         w1s = sbt("w1s", [P, E, K], U8)
         wps = sbt("wps", [P, E, K], U8)
         gcol = sbt("gcol", [P, CHUNKS], F32)
         ident = sbt("ident", [P, P], F32)
-        win = [[sbt("win%d_%d" % (a, b), [P, T], F32) for b in range(2)] for a in range(2)]
+        win = [[sbt("win%d_%d" % (a, b), [P, T], F32) for b in range(3 - a)] for a in range(2)]
 
-        nc.gpsimd.memset(dys[:].bitcast(I32), 0)
-        nc.gpsimd.memset(w2s[:].bitcast(I32), 0)
-        nc.gpsimd.memset(w1s[:].bitcast(I32), 0)
-        nc.gpsimd.memset(wps[:].bitcast(I32), 0)
+        def window(a, kb):
+            return win[a][kb % len(win[a])]
+
+
+        nc.vector.memset(dys[:].bitcast(I32), 0)
         nc.vector.memset(win[0][0][:], 0.0)
-        nc.vector.memset(win[1][0][:], 0.0)
         nc.vector.memset(win[0][1][:], 0.0)
+        nc.gpsimd.memset(win[1][0][:], 0.0)
         make_identity(nc, ident[:])
+        nc.gpsimd.memset(win[1][1][:], 0.0)
 
-        def load_scales(queue, plane, scales):
+        def load_scales(queue, plane, scales, which):
             rows = scales.rearrange("e s (q r) i -> r q (e s) i", r=4)
-            for r in range(4):
+            for r in which:
                 queue.dma_start(out=plane[:].bitcast(I32)[r:P:32], in_=rows[r].bitcast(I32))
 
         def words_of(w):
             return w.rearrange("e s p i d -> p (e s) (i d)").bitcast(I32)
 
         nc.sync.dma_start(idx[:], offs)
-        dy_rows = dy_scales[0].rearrange("(q r) t -> r q t", r=4)
-        for r in range(4):
-            nc.scalar.dma_start(out=dys[:].bitcast(I32)[r:P:32], in_=dy_rows[r].bitcast(I32))
+        load_scales(nc.scalar, w2s, w2t_scales, [0])
+        load_scales(nc.sync, w2s, w2t_scales, [1])
+        load_scales(nc.scalar, w2s, w2t_scales, [2])
         nc.sync.dma_start(out=dyw[:], in_=dy_words[0].rearrange("p t d -> p (t d)").bitcast(I32))
+        load_scales(nc.scalar, w2s, w2t_scales, [3])
         nc.sync.dma_start(out=w2w[0][:], in_=words_of(w2t_words)[:, 0, :])
         with nc.allow_non_contiguous_dma(reason="one gate value a partition"):
-            nc.sync.dma_start(out=gcol[:], in_=gate[0:1, :].rearrange("o (c p) -> p (o c)", p=P))
-        load_scales(nc.sync, w2s, w2t_scales)
-        nc.sync.dma_start(out=w1w[:], in_=words_of(w1t_words))
-        load_scales(nc.sync, w1s, w1t_scales)
+            nc.scalar.dma_start(out=gcol[:], in_=gate[0:1, :].rearrange("o (c p) -> p (o c)", p=P))
+        dy_rows = dy_scales[0].rearrange("(q r) t -> r q t", r=4)
+        for r in range(4):
+            nc.sync.dma_start(out=dys[:].bitcast(I32)[r:P:32], in_=dy_rows[r].bitcast(I32))
+        nc.sync.dma_start(out=w1w[0][:], in_=words_of(w1t_words)[:, 0, :])
+        load_scales(nc.sync, w1s, w1t_scales, range(4))
         nc.sync.dma_start(out=w2w[1][:], in_=words_of(w2t_words)[:, 1, :])
+        nc.sync.dma_start(out=w1w[1][:], in_=words_of(w1t_words)[:, 1, :])
         nc.sync.dma_start(out=wpw[:], in_=words_of(wpt_words))
+        load_scales(nc.sync, wps, wpt_scales, range(4))
         nc.sync.dma_start(idx2[:], offs2)
-        load_scales(nc.sync, wps, wpt_scales)
 
-        nc.scalar.activation(out=win[1][1][:], in_=win[0][0][:], func=COPY)
+        nc.scalar.activation(out=win[0][2][:], in_=win[1][0][:], func=COPY)
 
         dq = sbt("dq", [P, S], U32)
         dqs = sbt("dqs", [P, S], U8)
-        gw = [sbt("gw%d" % c, [P, P], U32) for c in range(CHUNKS)]
+        gw = [sbt("gw%d" % c, [P, P], U32) for c in range(2)]
         gs = [sbt("gs%d" % c, [P, P], U8) for c in range(CHUNKS)]
         dh = [sbt("dh%d" % c, [P, H], BF16) for c in range(CHUNKS)]
         dht = [sbt("dht%d" % c, [P, P * 4], BF16) for c in range(CHUNKS)]
         lists = [idx, idx2]
-        words2 = [w1w, wpw]
+        words2 = [[w1w[e][:] for e in range(E)], [wpw[:, e, :] for e in range(E)]]
         scales2 = [w1s, wps]
         src = [[sbt("src%d_%d" % (a, kb), [P, S], F32) for kb in range(KBLOCKS)] for a in range(2)]
 
         def gather(c):
             cols = idx[:, c * 8 : (c + 1) * 8]
+            nc.vector.tensor_copy(gw[c % 2][:], dyw[:].bitcast(U32).indirect(cols))
             nc.vector.tensor_copy(gs[c][:], dys[:].indirect(cols))
-            nc.vector.tensor_copy(gw[c][:], dyw[:].bitcast(U32).indirect(cols))
 
         def first(c):
             e = c * P // C
             acc = banks[c % 2]
             nc.tensor.matmul_mx(
-                out=acc[:], lhsT=gw[c][:].bitcast(X4), lhsT_scale=gs[c][:],
+                out=acc[:], lhsT=gw[c % 2][:].bitcast(X4), lhsT_scale=gs[c][:],
                 rhs=w2w[e][:].bitcast(X4), rhs_scale=w2s[:, e, :], start=True, stop=True,
             )
             nc.scalar.activation(
@@ -130,13 +136,13 @@ def tile_moe_dub_none_kernel(
                 e = s0 // C
                 nc.tensor.matmul_mx(
                     out=bank[:, s0 - lo : s0 - lo + step],
-                    lhsT=words2[a][:, e, kb * P : (kb + 1) * P].bitcast(X4),
+                    lhsT=words2[a][e][:, kb * P : (kb + 1) * P].bitcast(X4),
                     lhsT_scale=scales2[a][:, e, kb * P : (kb + 1) * P],
                     rhs=dq[:, s0 : s0 + step].bitcast(X4), rhs_scale=dqs[:, s0 : s0 + step],
                     start=True, stop=True,
                 )
             nc.scalar.copy(out=src[a][kb][:, lo:hi], in_=bank[:, 0 : hi - lo])
-            nc.vector.tensor_copy(win[a][kb % 2][:].indirect(lists[a][:, lo // 16 : hi // 16]), src[a][kb][:, lo:hi])
+            nc.vector.tensor_copy(window(a, kb)[:].indirect(lists[a][:, lo // 16 : hi // 16]), src[a][kb][:, lo:hi])
 
         def add_on_tensor(kb):
             half = T // 2
@@ -147,48 +153,49 @@ def tile_moe_dub_none_kernel(
                     cols = slice(h * half + j * P, h * half + (j + 1) * P)
                     for a in range(2):
                         nc.tensor.matmul(
-                            banks[h][:, j * P : (j + 1) * P], lhsT=win[a][kb % 2][:, cols], rhs=ident[:],
+                            banks[h][:, j * P : (j + 1) * P], lhsT=window(a, kb)[:, cols], rhs=ident[:],
                             is_transpose=True, start=(a == 0), stop=(a == 1),
                         )
                 nc.scalar.copy(out=turned[:], in_=banks[h][:, 0:half])
                 for j in range(half // P):
                     nc.tensor.transpose(banks[2 + h][:, j * P : (j + 1) * P], turned[:, j * P : (j + 1) * P], ident[:])
                 nc.scalar.copy(out=res[:, h * half : (h + 1) * half], in_=banks[2 + h][:, 0:half])
-            nc.sync.dma_start(out=out[kb * P : (kb + 1) * P, :], in_=res[:])
+            nc.scalar.dma_start(out=out[kb * P : (kb + 1) * P, :], in_=res[:])
 
         def add_on_vector(kb):
             third = T // 3
             for j in range(3):
                 cols = slice(j * third, (j + 1) * third)
                 res = sbt("res%d_%d" % (kb, j), [P, third], F32)
-                nc.vector.tensor_tensor(res[:], win[0][kb % 2][:, cols], win[1][kb % 2][:, cols], ADD)
-                queue = nc.scalar if j == 1 else nc.sync
-                queue.dma_start(out=out[kb * P : (kb + 1) * P, cols], in_=res[:])
+                nc.vector.tensor_tensor(res[:], window(0, kb)[:, cols], window(1, kb)[:, cols], ADD)
+                nc.sync.dma_start(out=out[kb * P : (kb + 1) * P, cols], in_=res[:])
 
-        for c in range(CHUNKS):
-            gather(c)
+        gather(0)
+        gather(1)
         first(0)
+        gather(2)
         first(1)
+        gather(3)
         turn(0)
         second(0, 0, 0, P, banks[4])
         turn(1)
-        second(1, 0, 0, P, banks[5])
+        second(0, 1, 0, P, banks[5])
         first(2)
         second(0, 0, P, C, banks[6])
         turn(2)
         first(3)
-        second(1, 0, P, C, banks[7])
+        second(0, 1, P, C, banks[7])
         turn(3)
-        second(0, 1, 0, C, banks[3])
+        second(0, 2, 0, C, banks[3])
         second(0, 0, C, S, banks[4])
-        second(1, 0, C, S, banks[5])
+        second(1, 0, 0, S, banks[5])
         second(0, 1, C, S, banks[6])
         second(1, 1, 0, S, banks[7])
         add_on_tensor(0)
-        second(0, 2, 0, S, banks[4])
+        second(0, 2, C, S, banks[4])
         second(1, 2, 0, S, banks[5])
         add_on_tensor(1)
-        second(0, 3, 0, S, banks[6])
+        second(0, 3, 0, S, banks[5])
         second(1, 3, 0, S, banks[7])
         add_on_tensor(2)
         add_on_vector(3)

@@ -17,6 +17,7 @@ U8 = mybir.dt.uint8
 X4 = mybir.dt.float8_e4m3fn_x4
 COPY = mybir.ActivationFunctionType.Copy
 ADD = mybir.AluOpType.add
+MULT = mybir.AluOpType.mult
 
 CHUNKS = S // P
 KBLOCKS = K // P
@@ -53,7 +54,6 @@ def tile_moe_dub_none_kernel(
             return win[a][kb % len(win[a])]
 
 
-        nc.vector.memset(dys[:].bitcast(I32), 0)
         nc.vector.memset(win[0][0][:], 0.0)
         nc.vector.memset(win[0][1][:], 0.0)
         nc.gpsimd.memset(win[1][0][:], 0.0)
@@ -69,17 +69,21 @@ def tile_moe_dub_none_kernel(
             return w.rearrange("e s p i d -> p (e s) (i d)").bitcast(I32)
 
         nc.sync.dma_start(idx[:], offs)
-        load_scales(nc.scalar, w2s, w2t_scales, [0])
-        load_scales(nc.sync, w2s, w2t_scales, [1])
-        load_scales(nc.scalar, w2s, w2t_scales, [2])
+        dy_rows = dy_scales[0].bitcast(I32)
+
+        def load_dy_scales(queue, q):
+            rows = dy_rows[4 * q : 4 * q + 4, :].unsqueeze(0).to_broadcast([8, 4, T // 4])
+            queue.dma_start(out=dys[:].bitcast(I32)[32 * q : 32 * q + 32, :], in_=rows)
+
+        load_dy_scales(nc.scalar, 0)
+        load_dy_scales(nc.sync, 1)
+        load_dy_scales(nc.scalar, 2)
         nc.sync.dma_start(out=dyw[:], in_=dy_words[0].rearrange("p t d -> p (t d)").bitcast(I32))
-        load_scales(nc.scalar, w2s, w2t_scales, [3])
+        load_dy_scales(nc.scalar, 3)
         nc.sync.dma_start(out=w2w[0][:], in_=words_of(w2t_words)[:, 0, :])
         with nc.allow_non_contiguous_dma(reason="one gate value a partition"):
             nc.scalar.dma_start(out=gcol[:], in_=gate[0:1, :].rearrange("o (c p) -> p (o c)", p=P))
-        dy_rows = dy_scales[0].rearrange("(q r) t -> r q t", r=4)
-        for r in range(4):
-            nc.sync.dma_start(out=dys[:].bitcast(I32)[r:P:32], in_=dy_rows[r].bitcast(I32))
+        load_scales(nc.sync, w2s, w2t_scales, range(4))
         nc.sync.dma_start(out=w1w[0][:], in_=words_of(w1t_words)[:, 0, :])
         load_scales(nc.sync, w1s, w1t_scales, range(4))
         nc.sync.dma_start(out=w2w[1][:], in_=words_of(w2t_words)[:, 1, :])
@@ -93,7 +97,7 @@ def tile_moe_dub_none_kernel(
         dq = sbt("dq", [P, S], U32)
         dqs = sbt("dqs", [P, S], U8)
         gw = [sbt("gw%d" % c, [P, P], U32) for c in range(2)]
-        gs = [sbt("gs%d" % c, [P, P], U8) for c in range(CHUNKS)]
+        gs = sbt("gs", [P, C], U8)
         dh = [sbt("dh%d" % c, [P, H], BF16) for c in range(CHUNKS)]
         dht = [sbt("dht%d" % c, [P, P * 4], BF16) for c in range(CHUNKS)]
         lists = [idx, idx2]
@@ -104,13 +108,28 @@ def tile_moe_dub_none_kernel(
         def gather(c):
             cols = idx[:, c * 8 : (c + 1) * 8]
             nc.vector.tensor_copy(gw[c % 2][:], dyw[:].bitcast(U32).indirect(cols))
-            nc.vector.tensor_copy(gs[c][:], dys[:].indirect(cols))
 
-        def first(c):
+        def gather_scales(e):
+            nc.vector.tensor_copy(gs[:], dys[:].indirect(idx[:, e * 16 : (e + 1) * 16]))
+
+        def first_split(c, left, right):
             e = c * P // C
-            acc = banks[c % 2]
+            half = H // 2
+            paired = dh[c][:].rearrange("s (u p h) -> s u p h", u=2, h=2)
+            for j, acc in enumerate((left, right)):
+                nc.tensor.matmul_mx(
+                    out=acc[:, 0:half], lhsT=gw[c % 2][:].bitcast(X4), lhsT_scale=gs[:, c % 2 * P : (c % 2 + 1) * P],
+                    rhs=w2w[e][:, j * half : (j + 1) * half].bitcast(X4), rhs_scale=w2s[:, e, j * half : (j + 1) * half],
+                    start=True, stop=True,
+                )
+            sums = [acc[:, 0:half].rearrange("s (p u h) -> s u p h", u=2, h=2) for acc in (left, right)]
+            nc.scalar.activation(out=paired[:, :, 0 : P // 2, :], in_=sums[0], func=COPY, scale=gcol[:, c : c + 1])
+            nc.vector.tensor_scalar(paired[:, :, P // 2 : P, :], sums[1], gcol[:, c : c + 1], None, MULT)
+
+        def first(c, acc):
+            e = c * P // C
             nc.tensor.matmul_mx(
-                out=acc[:], lhsT=gw[c % 2][:].bitcast(X4), lhsT_scale=gs[c][:],
+                out=acc[:], lhsT=gw[c % 2][:].bitcast(X4), lhsT_scale=gs[:, c % 2 * P : (c % 2 + 1) * P],
                 rhs=w2w[e][:].bitcast(X4), rhs_scale=w2s[:, e, :], start=True, stop=True,
             )
             nc.scalar.activation(
@@ -130,7 +149,7 @@ def tile_moe_dub_none_kernel(
             )
             nc.vector.quantize_mx(out=dq[:, c * P : (c + 1) * P].bitcast(X4), scales=dqs[:, c * P : (c + 1) * P], in_=dht[c][:])
 
-        def second(a, kb, lo, hi, bank):
+        def product(a, kb, lo, hi, bank):
             step = min(hi - lo, C)
             for s0 in range(lo, hi, step):
                 e = s0 // C
@@ -142,7 +161,13 @@ def tile_moe_dub_none_kernel(
                     start=True, stop=True,
                 )
             nc.scalar.copy(out=src[a][kb][:, lo:hi], in_=bank[:, 0 : hi - lo])
+
+        def scatter(a, kb, lo, hi):
             nc.vector.tensor_copy(window(a, kb)[:].indirect(lists[a][:, lo // 16 : hi // 16]), src[a][kb][:, lo:hi])
+
+        def second(a, kb, lo, hi, bank):
+            product(a, kb, lo, hi, bank)
+            scatter(a, kb, lo, hi)
 
         def add_on_tensor(kb):
             half = T // 2
@@ -151,10 +176,10 @@ def tile_moe_dub_none_kernel(
                 turned = sbt("turned%d_%d" % (kb, h), [P, half], F32)
                 for j in range(half // P):
                     cols = slice(h * half + j * P, h * half + (j + 1) * P)
-                    for a in range(2):
+                    for a in (1, 0):
                         nc.tensor.matmul(
                             banks[h][:, j * P : (j + 1) * P], lhsT=window(a, kb)[:, cols], rhs=ident[:],
-                            is_transpose=True, start=(a == 0), stop=(a == 1),
+                            is_transpose=True, start=(a == 1), stop=(a == 0),
                         )
                 nc.scalar.copy(out=turned[:], in_=banks[h][:, 0:half])
                 for j in range(half // P):
@@ -170,32 +195,37 @@ def tile_moe_dub_none_kernel(
                 nc.vector.tensor_tensor(res[:], window(0, kb)[:, cols], window(1, kb)[:, cols], ADD)
                 nc.sync.dma_start(out=out[kb * P : (kb + 1) * P, cols], in_=res[:])
 
+        gather_scales(0)
         gather(0)
         gather(1)
-        first(0)
+        first_split(0, banks[0], banks[1])
         gather(2)
-        first(1)
+        first(1, banks[6])
+        gather_scales(1)
         gather(3)
         turn(0)
         second(0, 0, 0, P, banks[4])
         turn(1)
         second(0, 1, 0, P, banks[5])
-        first(2)
+        first(2, banks[0])
         second(0, 0, P, C, banks[6])
         turn(2)
-        first(3)
+        first(3, banks[1])
         second(0, 1, P, C, banks[7])
         turn(3)
         second(0, 2, 0, C, banks[3])
         second(0, 0, C, S, banks[4])
-        second(1, 0, 0, S, banks[5])
-        second(0, 1, C, S, banks[6])
-        second(1, 1, 0, S, banks[7])
+        second(0, 1, C, S, banks[5])
+        second(0, 2, C, S, banks[6])
+        product(0, 3, 0, S, banks[7])
+        for kb in range(KBLOCKS):
+            product(1, kb, 0, S, banks[4 + kb])
+        scatter(1, 0, 0, S)
+        scatter(1, 1, 0, S)
         add_on_tensor(0)
-        second(0, 2, C, S, banks[4])
-        second(1, 2, 0, S, banks[5])
+        scatter(1, 2, 0, S)
+        scatter(0, 3, 0, S)
         add_on_tensor(1)
-        second(0, 3, 0, S, banks[5])
-        second(1, 3, 0, S, banks[7])
+        scatter(1, 3, 0, S)
         add_on_tensor(2)
         add_on_vector(3)

@@ -6,7 +6,7 @@ from concourse.masks import make_identity
 K, T, E, C, H, N = 512, 768, 2, 256, 512, 512
 S = E * C
 P = 128
-FLOPS = 3 * 2 * 512 * 512 * S
+FLOPS = 2 * S * (N * H + 2 * H * K)
 
 F32 = mybir.dt.float32
 BF16 = mybir.dt.bfloat16
@@ -20,7 +20,14 @@ ADD = mybir.AluOpType.add
 MULT = mybir.AluOpType.mult
 
 CHUNKS = S // P
-KBLOCKS = K // P
+ROW_BLOCKS = K // P
+LIST_ROWS = 16
+QUAD = 32
+QUAD_BLOCKS = 4
+BANK = 512
+DX, DP = 0, 1
+WINDOWS = (3, 2)
+LAST_PIECES = 3
 
 
 def tile_moe_dub_none_kernel(
@@ -31,201 +38,217 @@ def tile_moe_dub_none_kernel(
         sb = ctx.enter_context(tc.tile_pool(name="sb", bufs=1))
         ps = ctx.enter_context(tc.psum_pool(name="ps", bufs=1))
 
-        def sbt(name, shape, dtype):
+        def sbuf(name, shape, dtype):
             return sb.tile(shape, dtype, name=name, align_bytes=64)
 
-        idx = sb.tile([P, S // 16], U16, name="idx")
-        idx2 = sb.tile([P, S // 16], U16, name="idx2")
-        banks = [ps.tile([P, 512], F32, name="bank%d" % b) for b in range(8)]
+        idx = sb.tile([P, S // LIST_ROWS], U16, name="idx")
+        idx2 = sb.tile([P, S // LIST_ROWS], U16, name="idx2")
+        banks = [ps.tile([P, BANK], F32, name="bank%d" % b) for b in range(8)]
+        sum_banks, turn_banks, out_banks = banks[0:2], banks[2:4], banks[4:8]
 
-        dyw = sbt("dyw", [P, T], I32)
-        dys = sbt("dys", [P, T], U8)
-        w2w = [sbt("w2w%d" % e, [P, H], I32) for e in range(E)]
-        w1w = [sbt("w1w%d" % e, [P, K], I32) for e in range(E)]
-        wpw = sbt("wpw", [P, E, K], I32)
-        w2s = sbt("w2s", [P, E, H], U8)
-        w1s = sbt("w1s", [P, E, K], U8)
-        wps = sbt("wps", [P, E, K], U8)
-        gcol = sbt("gcol", [P, CHUNKS], F32)
-        ident = sbt("ident", [P, P], F32)
-        win = [[sbt("win%d_%d" % (a, b), [P, T], F32) for b in range(3 - a)] for a in range(2)]
+        dy_w = sbuf("dy_w", [P, T], I32)
+        dy_s = sbuf("dy_s", [P, T], U8)
+        w2_w = [sbuf("w2_w%d" % e, [P, H], I32) for e in range(E)]
+        w1_w = [sbuf("w1_w%d" % e, [P, K], I32) for e in range(E)]
+        wp_w = sbuf("wp_w", [P, E, K], I32)
+        w2_s = sbuf("w2_s", [P, E, H], U8)
+        w1_s = sbuf("w1_s", [P, E, K], U8)
+        wp_s = sbuf("wp_s", [P, E, K], U8)
+        gate_col = sbuf("gate_col", [P, CHUNKS], F32)
+        ident = sbuf("ident", [P, P], F32)
+        windows = [[sbuf("window%d_%d" % (which, b), [P, T], F32) for b in range(WINDOWS[which])] for which in (DX, DP)]
 
-        def window(a, kb):
-            return win[a][kb % len(win[a])]
+        def window(which, kb):
+            return windows[which][kb % WINDOWS[which]]
 
-
-        nc.vector.memset(win[0][0][:], 0.0)
-        nc.vector.memset(win[0][1][:], 0.0)
-        nc.gpsimd.memset(win[1][0][:], 0.0)
+        nc.vector.memset(windows[DX][0][:], 0.0)
+        nc.vector.memset(windows[DX][1][:], 0.0)
+        nc.gpsimd.memset(windows[DP][0][:], 0.0)
         make_identity(nc, ident[:])
-        nc.gpsimd.memset(win[1][1][:], 0.0)
+        nc.gpsimd.memset(windows[DP][1][:], 0.0)
 
-        def load_scales(queue, plane, scales, which):
-            rows = scales.rearrange("e s (q r) i -> r q (e s) i", r=4)
-            for r in which:
-                queue.dma_start(out=plane[:].bitcast(I32)[r:P:32], in_=rows[r].bitcast(I32))
+        def load_weight_scales(tile, scales, which_rows):
+            rows = scales.rearrange("e s (q r) i -> r q (e s) i", r=QUAD_BLOCKS)
+            for r in which_rows:
+                nc.sync.dma_start(out=tile[:].bitcast(I32)[r:P:QUAD], in_=rows[r].bitcast(I32))
 
         def words_of(w):
             return w.rearrange("e s p i d -> p (e s) (i d)").bitcast(I32)
 
-        nc.sync.dma_start(idx[:], offs)
-        dy_rows = dy_scales[0].bitcast(I32)
-
         def load_dy_scales(queue, q):
-            rows = dy_rows[4 * q : 4 * q + 4, :].unsqueeze(0).to_broadcast([8, 4, T // 4])
-            queue.dma_start(out=dys[:].bitcast(I32)[32 * q : 32 * q + 32, :], in_=rows)
+            rows = dy_scales[0].bitcast(I32)[QUAD_BLOCKS * q : QUAD_BLOCKS * (q + 1), :]
+            repeated = rows.unsqueeze(0).to_broadcast([QUAD // QUAD_BLOCKS, QUAD_BLOCKS, T // 4])
+            queue.dma_start(out=dy_s[:].bitcast(I32)[QUAD * q : QUAD * (q + 1), :], in_=repeated)
 
+        nc.sync.dma_start(idx[:], offs)
         load_dy_scales(nc.scalar, 0)
         load_dy_scales(nc.sync, 1)
         load_dy_scales(nc.scalar, 2)
-        nc.sync.dma_start(out=dyw[:], in_=dy_words[0].rearrange("p t d -> p (t d)").bitcast(I32))
+        load_weight_scales(w2_s, w2t_scales, range(0, 1))
         load_dy_scales(nc.scalar, 3)
-        nc.sync.dma_start(out=w2w[0][:], in_=words_of(w2t_words)[:, 0, :])
-        with nc.allow_non_contiguous_dma(reason="one gate value a partition"):
-            nc.scalar.dma_start(out=gcol[:], in_=gate[0:1, :].rearrange("o (c p) -> p (o c)", p=P))
-        load_scales(nc.sync, w2s, w2t_scales, range(4))
-        nc.sync.dma_start(out=w1w[0][:], in_=words_of(w1t_words)[:, 0, :])
-        load_scales(nc.sync, w1s, w1t_scales, range(4))
-        nc.sync.dma_start(out=w2w[1][:], in_=words_of(w2t_words)[:, 1, :])
-        nc.sync.dma_start(out=w1w[1][:], in_=words_of(w1t_words)[:, 1, :])
-        nc.sync.dma_start(out=wpw[:], in_=words_of(wpt_words))
-        load_scales(nc.sync, wps, wpt_scales, range(4))
+        nc.sync.dma_start(out=dy_w[:], in_=dy_words[0].rearrange("p t d -> p (t d)").bitcast(I32))
+        nc.sync.dma_start(out=w2_w[0][:], in_=words_of(w2t_words)[:, 0, :])
+        load_weight_scales(w2_s, w2t_scales, range(1, 4))
+        with nc.allow_non_contiguous_dma(reason="one gate value a partition and chunk"):
+            nc.sync.dma_start(out=gate_col[:], in_=gate[0:1, :].rearrange("o (c p) -> p (o c)", p=P))
+        load_weight_scales(w1_s, w1t_scales, range(0, 2))
+        nc.sync.dma_start(out=w1_w[0][:], in_=words_of(w1t_words)[:, 0, :])
+        load_weight_scales(w1_s, w1t_scales, range(2, 4))
+        nc.sync.dma_start(out=w2_w[1][:], in_=words_of(w2t_words)[:, 1, :])
+        nc.sync.dma_start(out=w1_w[1][:], in_=words_of(w1t_words)[:, 1, :])
+        nc.sync.dma_start(out=wp_w[:], in_=words_of(wpt_words))
+        load_weight_scales(wp_s, wpt_scales, range(0, 4))
         nc.sync.dma_start(idx2[:], offs2)
 
-        nc.scalar.activation(out=win[0][2][:], in_=win[1][0][:], func=COPY)
+        nc.scalar.activation(out=windows[DX][2][:], in_=windows[DP][0][:], func=COPY)
 
-        dq = sbt("dq", [P, S], U32)
-        dqs = sbt("dqs", [P, S], U8)
-        gw = [sbt("gw%d" % c, [P, P], U32) for c in range(2)]
-        gs = sbt("gs", [P, C], U8)
-        dh = [sbt("dh%d" % c, [P, H], BF16) for c in range(CHUNKS)]
-        dht = [sbt("dht%d" % c, [P, P * 4], BF16) for c in range(CHUNKS)]
+        dh_w = sbuf("dh_w", [P, S], U32)
+        dh_s = sbuf("dh_s", [P, S], U8)
+        slot_w = [sbuf("slot_w%d" % b, [P, P], U32) for b in range(2)]
+        slot_s = sbuf("slot_s", [P, C], U8)
+        dh_rows = [sbuf("dh_rows%d" % c, [P, H], BF16) for c in range(CHUNKS)]
+        dh_cols = [sbuf("dh_cols%d" % c, [P, P * 4], BF16) for c in range(CHUNKS)]
         lists = [idx, idx2]
-        words2 = [[w1w[e][:] for e in range(E)], [wpw[:, e, :] for e in range(E)]]
-        scales2 = [w1s, wps]
-        src = [[sbt("src%d_%d" % (a, kb), [P, S], F32) for kb in range(KBLOCKS)] for a in range(2)]
+        second_w = [[w1_w[e][:] for e in range(E)], [wp_w[:, e, :] for e in range(E)]]
+        second_s = [w1_s, wp_s]
+        staged = [[sbuf("staged%d_%d" % (which, kb), [P, S], F32) for kb in range(ROW_BLOCKS)] for which in (DX, DP)]
 
-        def gather(c):
-            cols = idx[:, c * 8 : (c + 1) * 8]
-            nc.vector.tensor_copy(gw[c % 2][:], dyw[:].bitcast(U32).indirect(cols))
+        def entries(which, lo, hi):
+            return lists[which][:, lo // LIST_ROWS : hi // LIST_ROWS]
+
+        def gather_words(c):
+            nc.vector.tensor_copy(slot_w[c % 2][:], dy_w[:].bitcast(U32).indirect(entries(DX, c * P, (c + 1) * P)))
 
         def gather_scales(e):
-            nc.vector.tensor_copy(gs[:], dys[:].indirect(idx[:, e * 16 : (e + 1) * 16]))
+            nc.vector.tensor_copy(slot_s[:], dy_s[:].indirect(entries(DX, e * C, (e + 1) * C)))
 
-        def first_split(c, left, right):
-            e = c * P // C
-            half = H // 2
-            paired = dh[c][:].rearrange("s (u p h) -> s u p h", u=2, h=2)
-            for j, acc in enumerate((left, right)):
-                nc.tensor.matmul_mx(
-                    out=acc[:, 0:half], lhsT=gw[c % 2][:].bitcast(X4), lhsT_scale=gs[:, c % 2 * P : (c % 2 + 1) * P],
-                    rhs=w2w[e][:, j * half : (j + 1) * half].bitcast(X4), rhs_scale=w2s[:, e, j * half : (j + 1) * half],
-                    start=True, stop=True,
-                )
-            sums = [acc[:, 0:half].rearrange("s (p u h) -> s u p h", u=2, h=2) for acc in (left, right)]
-            nc.scalar.activation(out=paired[:, :, 0 : P // 2, :], in_=sums[0], func=COPY, scale=gcol[:, c : c + 1])
-            nc.vector.tensor_scalar(paired[:, :, P // 2 : P, :], sums[1], gcol[:, c : c + 1], None, MULT)
-
-        def first(c, acc):
-            e = c * P // C
+        def first_product(c, lo, hi, bank):
+            e, place = divmod(c * P, C)
             nc.tensor.matmul_mx(
-                out=acc[:], lhsT=gw[c % 2][:].bitcast(X4), lhsT_scale=gs[:, c % 2 * P : (c % 2 + 1) * P],
-                rhs=w2w[e][:].bitcast(X4), rhs_scale=w2s[:, e, :], start=True, stop=True,
-            )
-            nc.scalar.activation(
-                out=dh[c][:].rearrange("s (u p h) -> s u p h", u=2, h=2),
-                in_=acc[:].rearrange("s (p u h) -> s u p h", u=2, h=2),
-                func=COPY, scale=gcol[:, c : c + 1],
+                out=bank[:, 0 : hi - lo],
+                lhsT=slot_w[c % 2][:].bitcast(X4),
+                lhsT_scale=slot_s[:, place : place + P],
+                rhs=w2_w[e][:, lo:hi].bitcast(X4),
+                rhs_scale=w2_s[:, e, lo:hi],
+                start=True,
+                stop=True,
             )
 
-        def turn(c):
-            bank = banks[2 + c % 2]
-            pairs = dh[c][:].bitcast(F32)
+        def by_pairs(c, lo, hi, bank):
+            dst = dh_rows[c][:].rearrange("s (u p h) -> s u p h", u=2, h=2)[:, :, lo // 4 : hi // 4, :]
+            src = bank[:, 0 : hi - lo].rearrange("s (p u h) -> s u p h", u=2, h=2)
+            return dst, src
+
+        def hidden(c, bank):
+            first_product(c, 0, H, bank)
+            dst, src = by_pairs(c, 0, H, bank)
+            nc.scalar.activation(out=dst, in_=src, func=COPY, scale=gate_col[:, c : c + 1])
+
+        def hidden_on_two_engines(c):
+            half = H // 2
+            first_product(c, 0, half, sum_banks[0])
+            first_product(c, half, H, sum_banks[1])
+            dst, src = by_pairs(c, 0, half, sum_banks[0])
+            nc.scalar.activation(out=dst, in_=src, func=COPY, scale=gate_col[:, c : c + 1])
+            dst, src = by_pairs(c, half, H, sum_banks[1])
+            nc.vector.tensor_scalar(dst, src, gate_col[:, c : c + 1], None, MULT)
+
+        def turn_and_quantise(c):
+            bank = turn_banks[c % 2]
+            pairs = dh_rows[c][:].bitcast(F32)
             for u in range(2):
                 nc.tensor.transpose(bank[:, u * P : (u + 1) * P], pairs[:, u * P : (u + 1) * P], ident[:])
             nc.scalar.copy(
-                out=dht[c][:].bitcast(F32).rearrange("p (s u) -> p s u", u=2),
+                out=dh_cols[c][:].bitcast(F32).rearrange("p (s u) -> p s u", u=2),
                 in_=bank[:, 0 : 2 * P].rearrange("p (u s) -> p s u", u=2),
             )
-            nc.vector.quantize_mx(out=dq[:, c * P : (c + 1) * P].bitcast(X4), scales=dqs[:, c * P : (c + 1) * P], in_=dht[c][:])
+            slots = slice(c * P, (c + 1) * P)
+            nc.vector.quantize_mx(out=dh_w[:, slots].bitcast(X4), scales=dh_s[:, slots], in_=dh_cols[c][:])
 
-        def product(a, kb, lo, hi, bank):
-            step = min(hi - lo, C)
-            for s0 in range(lo, hi, step):
+        def second_product(which, kb, lo, hi, bank):
+            width = min(hi - lo, C)
+            rows = slice(kb * P, (kb + 1) * P)
+            for s0 in range(lo, hi, width):
                 e = s0 // C
                 nc.tensor.matmul_mx(
-                    out=bank[:, s0 - lo : s0 - lo + step],
-                    lhsT=words2[a][e][:, kb * P : (kb + 1) * P].bitcast(X4),
-                    lhsT_scale=scales2[a][:, e, kb * P : (kb + 1) * P],
-                    rhs=dq[:, s0 : s0 + step].bitcast(X4), rhs_scale=dqs[:, s0 : s0 + step],
-                    start=True, stop=True,
+                    out=bank[:, s0 - lo : s0 - lo + width],
+                    lhsT=second_w[which][e][:, rows].bitcast(X4),
+                    lhsT_scale=second_s[which][:, e, rows],
+                    rhs=dh_w[:, s0 : s0 + width].bitcast(X4),
+                    rhs_scale=dh_s[:, s0 : s0 + width],
+                    start=True,
+                    stop=True,
                 )
-            nc.scalar.copy(out=src[a][kb][:, lo:hi], in_=bank[:, 0 : hi - lo])
+            nc.scalar.copy(out=staged[which][kb][:, lo:hi], in_=bank[:, 0 : hi - lo])
 
-        def scatter(a, kb, lo, hi):
-            nc.vector.tensor_copy(window(a, kb)[:].indirect(lists[a][:, lo // 16 : hi // 16]), src[a][kb][:, lo:hi])
+        def scatter(which, kb, lo, hi):
+            nc.vector.tensor_copy(window(which, kb)[:].indirect(entries(which, lo, hi)), staged[which][kb][:, lo:hi])
 
-        def second(a, kb, lo, hi, bank):
-            product(a, kb, lo, hi, bank)
-            scatter(a, kb, lo, hi)
+        def dx_piece(kb, lo, hi, bank):
+            second_product(DX, kb, lo, hi, bank)
+            scatter(DX, kb, lo, hi)
 
         def add_on_tensor(kb):
             half = T // 2
-            res = sbt("res%d" % kb, [P, T], F32)
-            for h in range(2):
-                turned = sbt("turned%d_%d" % (kb, h), [P, half], F32)
+            total = sbuf("total%d" % kb, [P, T], F32)
+            for part in range(2):
+                turned = sbuf("turned%d_%d" % (kb, part), [P, half], F32)
                 for j in range(half // P):
-                    cols = slice(h * half + j * P, h * half + (j + 1) * P)
-                    for a in (1, 0):
+                    cols = slice(part * half + j * P, part * half + (j + 1) * P)
+                    for which in (DP, DX):
                         nc.tensor.matmul(
-                            banks[h][:, j * P : (j + 1) * P], lhsT=window(a, kb)[:, cols], rhs=ident[:],
-                            is_transpose=True, start=(a == 1), stop=(a == 0),
+                            sum_banks[part][:, j * P : (j + 1) * P],
+                            lhsT=window(which, kb)[:, cols],
+                            rhs=ident[:],
+                            is_transpose=True,
+                            start=(which == DP),
+                            stop=(which == DX),
                         )
-                nc.scalar.copy(out=turned[:], in_=banks[h][:, 0:half])
+                nc.scalar.copy(out=turned[:], in_=sum_banks[part][:, 0:half])
                 for j in range(half // P):
-                    nc.tensor.transpose(banks[2 + h][:, j * P : (j + 1) * P], turned[:, j * P : (j + 1) * P], ident[:])
-                nc.scalar.copy(out=res[:, h * half : (h + 1) * half], in_=banks[2 + h][:, 0:half])
-            nc.scalar.dma_start(out=out[kb * P : (kb + 1) * P, :], in_=res[:])
+                    nc.tensor.transpose(turn_banks[part][:, j * P : (j + 1) * P], turned[:, j * P : (j + 1) * P], ident[:])
+                nc.scalar.copy(out=total[:, part * half : (part + 1) * half], in_=turn_banks[part][:, 0:half])
+            nc.scalar.dma_start(out=out[kb * P : (kb + 1) * P, :], in_=total[:])
 
         def add_on_vector(kb):
-            third = T // 3
-            for j in range(3):
-                cols = slice(j * third, (j + 1) * third)
-                res = sbt("res%d_%d" % (kb, j), [P, third], F32)
-                nc.vector.tensor_tensor(res[:], window(0, kb)[:, cols], window(1, kb)[:, cols], ADD)
-                nc.sync.dma_start(out=out[kb * P : (kb + 1) * P, cols], in_=res[:])
+            width = T // LAST_PIECES
+            for j in range(LAST_PIECES):
+                cols = slice(j * width, (j + 1) * width)
+                total = sbuf("total%d_%d" % (kb, j), [P, width], F32)
+                nc.vector.tensor_tensor(total[:], window(DX, kb)[:, cols], window(DP, kb)[:, cols], ADD)
+                nc.sync.dma_start(out=out[kb * P : (kb + 1) * P, cols], in_=total[:])
 
         gather_scales(0)
-        gather(0)
-        gather(1)
-        first_split(0, banks[0], banks[1])
-        gather(2)
-        first(1, banks[6])
+        gather_words(0)
+        gather_words(1)
+        hidden_on_two_engines(0)
+        gather_words(2)
+        hidden(1, out_banks[2])
         gather_scales(1)
-        gather(3)
-        turn(0)
-        second(0, 0, 0, P, banks[4])
-        turn(1)
-        second(0, 1, 0, P, banks[5])
-        first(2, banks[0])
-        second(0, 0, P, C, banks[6])
-        turn(2)
-        first(3, banks[1])
-        second(0, 1, P, C, banks[7])
-        turn(3)
-        second(0, 2, 0, C, banks[3])
-        second(0, 0, C, S, banks[4])
-        second(0, 1, C, S, banks[5])
-        second(0, 2, C, S, banks[6])
-        product(0, 3, 0, S, banks[7])
-        for kb in range(KBLOCKS):
-            product(1, kb, 0, S, banks[4 + kb])
-        scatter(1, 0, 0, S)
-        scatter(1, 1, 0, S)
+        gather_words(3)
+        turn_and_quantise(0)
+        dx_piece(0, 0, P, out_banks[0])
+        turn_and_quantise(1)
+        dx_piece(1, 0, P, out_banks[1])
+        hidden(2, sum_banks[0])
+        dx_piece(0, P, C, out_banks[2])
+        turn_and_quantise(2)
+        hidden(3, sum_banks[1])
+        dx_piece(1, P, C, out_banks[3])
+        turn_and_quantise(3)
+        dx_piece(2, 0, C, turn_banks[1])
+        for kb in range(WINDOWS[DX]):
+            dx_piece(kb, C, S, out_banks[kb])
+        last = ROW_BLOCKS - 1
+        second_product(DX, last, 0, S, out_banks[last])
+        for kb in range(ROW_BLOCKS):
+            second_product(DP, kb, 0, S, out_banks[kb])
+        scatter(DP, 0, 0, S)
+        scatter(DP, 1, 0, S)
         add_on_tensor(0)
-        scatter(1, 2, 0, S)
-        scatter(0, 3, 0, S)
+        scatter(DP, 2, 0, S)
+        scatter(DX, last, 0, S)
         add_on_tensor(1)
-        scatter(1, 3, 0, S)
+        scatter(DP, last, 0, S)
         add_on_tensor(2)
-        add_on_vector(3)
+        add_on_vector(last)

from contextlib import ExitStack

import concourse.mybir as mybir
from concourse.masks import make_identity

K, T, E, C, H, N = 512, 768, 2, 256, 512, 512
S = E * C
P = 128
FLOPS = 2 * S * (N * H + 2 * H * K)

F32 = mybir.dt.float32
BF16 = mybir.dt.bfloat16
I32 = mybir.dt.int32
U32 = mybir.dt.uint32
U16 = mybir.dt.uint16
U8 = mybir.dt.uint8
X4 = mybir.dt.float8_e4m3fn_x4
COPY = mybir.ActivationFunctionType.Copy
ADD = mybir.AluOpType.add
MULT = mybir.AluOpType.mult

CHUNKS = S // P
ROW_BLOCKS = K // P
LIST_ROWS = 16
QUAD = 32
QUAD_BLOCKS = 4
BANK = 512
DX, DP = 0, 1
WINDOWS = (3, 2)
LAST_PIECES = 3


def tile_moe_dub_none_kernel(
    tc, dy_words, dy_scales, w2t_words, w2t_scales, w1t_words, w1t_scales, wpt_words, wpt_scales, gate, offs, offs2, out
):
    nc = tc.nc
    with ExitStack() as ctx:
        sb = ctx.enter_context(tc.tile_pool(name="sb", bufs=1))
        ps = ctx.enter_context(tc.psum_pool(name="ps", bufs=1))

        def sbuf(name, shape, dtype):
            return sb.tile(shape, dtype, name=name, align_bytes=64)

        idx = sb.tile([P, S // LIST_ROWS], U16, name="idx")
        idx2 = sb.tile([P, S // LIST_ROWS], U16, name="idx2")
        banks = [ps.tile([P, BANK], F32, name="bank%d" % b) for b in range(8)]
        sum_banks, turn_banks, out_banks = banks[0:2], banks[2:4], banks[4:8]

        dy_w = sbuf("dy_w", [P, T], I32)
        dy_s = sbuf("dy_s", [P, T], U8)
        w2_w = [sbuf("w2_w%d" % e, [P, H], I32) for e in range(E)]
        w1_w = [sbuf("w1_w%d" % e, [P, K], I32) for e in range(E)]
        wp_w = sbuf("wp_w", [P, E, K], I32)
        w2_s = sbuf("w2_s", [P, E, H], U8)
        w1_s = sbuf("w1_s", [P, E, K], U8)
        wp_s = sbuf("wp_s", [P, E, K], U8)
        gate_col = sbuf("gate_col", [P, CHUNKS], F32)
        ident = sbuf("ident", [P, P], F32)
        windows = [[sbuf("window%d_%d" % (which, b), [P, T], F32) for b in range(WINDOWS[which])] for which in (DX, DP)]

        def window(which, kb):
            return windows[which][kb % WINDOWS[which]]

        nc.vector.memset(windows[DX][0][:], 0.0)
        nc.vector.memset(windows[DX][1][:], 0.0)
        nc.gpsimd.memset(windows[DP][0][:], 0.0)
        make_identity(nc, ident[:])
        nc.gpsimd.memset(windows[DP][1][:], 0.0)

        def load_weight_scales(tile, scales, which_rows):
            rows = scales.rearrange("e s (q r) i -> r q (e s) i", r=QUAD_BLOCKS)
            for r in which_rows:
                nc.sync.dma_start(out=tile[:].bitcast(I32)[r:P:QUAD], in_=rows[r].bitcast(I32))

        def words_of(w):
            return w.rearrange("e s p i d -> p (e s) (i d)").bitcast(I32)

        def load_dy_scales(queue, q):
            rows = dy_scales[0].bitcast(I32)[QUAD_BLOCKS * q : QUAD_BLOCKS * (q + 1), :]
            repeated = rows.unsqueeze(0).to_broadcast([QUAD // QUAD_BLOCKS, QUAD_BLOCKS, T // 4])
            queue.dma_start(out=dy_s[:].bitcast(I32)[QUAD * q : QUAD * (q + 1), :], in_=repeated)

        nc.sync.dma_start(idx[:], offs)
        load_dy_scales(nc.scalar, 0)
        load_dy_scales(nc.sync, 1)
        load_dy_scales(nc.scalar, 2)
        load_weight_scales(w2_s, w2t_scales, range(0, 1))
        load_dy_scales(nc.scalar, 3)
        nc.sync.dma_start(out=dy_w[:], in_=dy_words[0].rearrange("p t d -> p (t d)").bitcast(I32))
        nc.sync.dma_start(out=w2_w[0][:], in_=words_of(w2t_words)[:, 0, :])
        load_weight_scales(w2_s, w2t_scales, range(1, 4))
        with nc.allow_non_contiguous_dma(reason="one gate value a partition and chunk"):
            nc.sync.dma_start(out=gate_col[:], in_=gate[0:1, :].rearrange("o (c p) -> p (o c)", p=P))
        load_weight_scales(w1_s, w1t_scales, range(0, 2))
        nc.sync.dma_start(out=w1_w[0][:], in_=words_of(w1t_words)[:, 0, :])
        load_weight_scales(w1_s, w1t_scales, range(2, 4))
        nc.sync.dma_start(out=w2_w[1][:], in_=words_of(w2t_words)[:, 1, :])
        nc.sync.dma_start(out=w1_w[1][:], in_=words_of(w1t_words)[:, 1, :])
        nc.sync.dma_start(out=wp_w[:], in_=words_of(wpt_words))
        load_weight_scales(wp_s, wpt_scales, range(0, 4))
        nc.sync.dma_start(idx2[:], offs2)

        nc.scalar.activation(out=windows[DX][2][:], in_=windows[DP][0][:], func=COPY)

        dh_w = sbuf("dh_w", [P, S], U32)
        dh_s = sbuf("dh_s", [P, S], U8)
        slot_w = [sbuf("slot_w%d" % b, [P, P], U32) for b in range(2)]
        slot_s = sbuf("slot_s", [P, C], U8)
        dh_rows = [sbuf("dh_rows%d" % c, [P, H], BF16) for c in range(CHUNKS)]
        dh_cols = [sbuf("dh_cols%d" % c, [P, P * 4], BF16) for c in range(CHUNKS)]
        lists = [idx, idx2]
        second_w = [[w1_w[e][:] for e in range(E)], [wp_w[:, e, :] for e in range(E)]]
        second_s = [w1_s, wp_s]
        staged = [[sbuf("staged%d_%d" % (which, kb), [P, S], F32) for kb in range(ROW_BLOCKS)] for which in (DX, DP)]

        def entries(which, lo, hi):
            return lists[which][:, lo // LIST_ROWS : hi // LIST_ROWS]

        def gather_words(c):
            nc.vector.tensor_copy(slot_w[c % 2][:], dy_w[:].bitcast(U32).indirect(entries(DX, c * P, (c + 1) * P)))

        def gather_scales(e):
            nc.vector.tensor_copy(slot_s[:], dy_s[:].indirect(entries(DX, e * C, (e + 1) * C)))

        def first_product(c, lo, hi, bank):
            e, place = divmod(c * P, C)
            nc.tensor.matmul_mx(
                out=bank[:, 0 : hi - lo],
                lhsT=slot_w[c % 2][:].bitcast(X4),
                lhsT_scale=slot_s[:, place : place + P],
                rhs=w2_w[e][:, lo:hi].bitcast(X4),
                rhs_scale=w2_s[:, e, lo:hi],
                start=True,
                stop=True,
            )

        def by_pairs(c, lo, hi, bank):
            dst = dh_rows[c][:].rearrange("s (u p h) -> s u p h", u=2, h=2)[:, :, lo // 4 : hi // 4, :]
            src = bank[:, 0 : hi - lo].rearrange("s (p u h) -> s u p h", u=2, h=2)
            return dst, src

        def hidden(c, bank):
            first_product(c, 0, H, bank)
            dst, src = by_pairs(c, 0, H, bank)
            nc.scalar.activation(out=dst, in_=src, func=COPY, scale=gate_col[:, c : c + 1])

        def hidden_on_two_engines(c):
            half = H // 2
            first_product(c, 0, half, sum_banks[0])
            first_product(c, half, H, sum_banks[1])
            dst, src = by_pairs(c, 0, half, sum_banks[0])
            nc.scalar.activation(out=dst, in_=src, func=COPY, scale=gate_col[:, c : c + 1])
            dst, src = by_pairs(c, half, H, sum_banks[1])
            nc.vector.tensor_scalar(dst, src, gate_col[:, c : c + 1], None, MULT)

        def turn_and_quantise(c):
            bank = turn_banks[c % 2]
            pairs = dh_rows[c][:].bitcast(F32)
            for u in range(2):
                nc.tensor.transpose(bank[:, u * P : (u + 1) * P], pairs[:, u * P : (u + 1) * P], ident[:])
            nc.scalar.copy(
                out=dh_cols[c][:].bitcast(F32).rearrange("p (s u) -> p s u", u=2),
                in_=bank[:, 0 : 2 * P].rearrange("p (u s) -> p s u", u=2),
            )
            slots = slice(c * P, (c + 1) * P)
            nc.vector.quantize_mx(out=dh_w[:, slots].bitcast(X4), scales=dh_s[:, slots], in_=dh_cols[c][:])

        def second_product(which, kb, lo, hi, bank):
            width = min(hi - lo, C)
            rows = slice(kb * P, (kb + 1) * P)
            for s0 in range(lo, hi, width):
                e = s0 // C
                nc.tensor.matmul_mx(
                    out=bank[:, s0 - lo : s0 - lo + width],
                    lhsT=second_w[which][e][:, rows].bitcast(X4),
                    lhsT_scale=second_s[which][:, e, rows],
                    rhs=dh_w[:, s0 : s0 + width].bitcast(X4),
                    rhs_scale=dh_s[:, s0 : s0 + width],
                    start=True,
                    stop=True,
                )
            nc.scalar.copy(out=staged[which][kb][:, lo:hi], in_=bank[:, 0 : hi - lo])

        def scatter(which, kb, lo, hi):
            nc.vector.tensor_copy(window(which, kb)[:].indirect(entries(which, lo, hi)), staged[which][kb][:, lo:hi])

        def dx_piece(kb, lo, hi, bank):
            second_product(DX, kb, lo, hi, bank)
            scatter(DX, kb, lo, hi)

        def add_on_tensor(kb):
            half = T // 2
            total = sbuf("total%d" % kb, [P, T], F32)
            for part in range(2):
                turned = sbuf("turned%d_%d" % (kb, part), [P, half], F32)
                for j in range(half // P):
                    cols = slice(part * half + j * P, part * half + (j + 1) * P)
                    for which in (DP, DX):
                        nc.tensor.matmul(
                            sum_banks[part][:, j * P : (j + 1) * P],
                            lhsT=window(which, kb)[:, cols],
                            rhs=ident[:],
                            is_transpose=True,
                            start=(which == DP),
                            stop=(which == DX),
                        )
                nc.scalar.copy(out=turned[:], in_=sum_banks[part][:, 0:half])
                for j in range(half // P):
                    nc.tensor.transpose(turn_banks[part][:, j * P : (j + 1) * P], turned[:, j * P : (j + 1) * P], ident[:])
                nc.scalar.copy(out=total[:, part * half : (part + 1) * half], in_=turn_banks[part][:, 0:half])
            nc.scalar.dma_start(out=out[kb * P : (kb + 1) * P, :], in_=total[:])

        def add_on_vector(kb):
            width = T // LAST_PIECES
            for j in range(LAST_PIECES):
                cols = slice(j * width, (j + 1) * width)
                total = sbuf("total%d_%d" % (kb, j), [P, width], F32)
                nc.vector.tensor_tensor(total[:], window(DX, kb)[:, cols], window(DP, kb)[:, cols], ADD)
                nc.sync.dma_start(out=out[kb * P : (kb + 1) * P, cols], in_=total[:])

        gather_scales(0)
        gather_words(0)
        gather_words(1)
        hidden_on_two_engines(0)
        gather_words(2)
        hidden(1, out_banks[2])
        gather_scales(1)
        gather_words(3)
        turn_and_quantise(0)
        dx_piece(0, 0, P, out_banks[0])
        turn_and_quantise(1)
        dx_piece(1, 0, P, out_banks[1])
        hidden(2, sum_banks[0])
        dx_piece(0, P, C, out_banks[2])
        turn_and_quantise(2)
        hidden(3, sum_banks[1])
        dx_piece(1, P, C, out_banks[3])
        turn_and_quantise(3)
        dx_piece(2, 0, C, turn_banks[1])
        for kb in range(WINDOWS[DX]):
            dx_piece(kb, C, S, out_banks[kb])
        last = ROW_BLOCKS - 1
        second_product(DX, last, 0, S, out_banks[last])
        for kb in range(ROW_BLOCKS):
            second_product(DP, kb, 0, S, out_banks[kb])
        scatter(DP, 0, 0, S)
        scatter(DP, 1, 0, S)
        add_on_tensor(0)
        scatter(DP, 2, 0, S)
        scatter(DX, last, 0, S)
        add_on_tensor(1)
        scatter(DP, last, 0, S)
        add_on_tensor(2)
        add_on_vector(last)
